import numpy as np
import ml_dtypes


def mxq(x, axis, fmt="e4m3"):
    dtype, down = {"e4m3": (ml_dtypes.float8_e4m3fn, 7), "e5m2": (ml_dtypes.float8_e5m2, 14)}[fmt]
    v = np.moveaxis(np.asarray(x, np.float32).astype(ml_dtypes.bfloat16).astype(np.float64), axis, -1)
    blocks = v.reshape(v.shape[:-1] + (-1, 32))
    amax = np.abs(blocks).max(-1, keepdims=True)
    byte = np.maximum(np.where(amax > 0, np.frexp(amax)[1] - 1 + 127, 0) - down, 1)
    scale = np.exp2(byte - 127.0)
    codes = (blocks / scale).astype(np.float32).astype(dtype).astype(np.float64)
    return np.moveaxis((codes * scale).reshape(v.shape), -1, axis)


WIDE = False


def mx_kscale(k):
    if not WIDE:
        return np.ones(k)
    levels = np.array([10, -10, 5, -5, 0])
    if k % 512:
        return np.exp2(np.random.permutation(np.resize(levels, k // 32))).repeat(32)
    a = np.empty((k // 512, 16))
    for p in range(k // 512):
        a[p, :8] = np.random.permutation(np.resize(levels, 8))
        for g in range(8):
            far = levels[np.abs(levels - a[p, g]) >= 10]
            a[p, g + 8] = far[np.random.randint(len(far))]
    return np.exp2(a.ravel()).repeat(32)


BF16 = ml_dtypes.bfloat16


def bf(x):
    return np.asarray(x, np.float32).astype(BF16)


def f64(x):
    return np.asarray(x).astype(np.float64)


E2M1 = np.array([0.0, 0.5, 1.0, 1.5, 2.0, 3.0, 4.0, 6.0, -0.0, -0.5, -1.0, -1.5, -2.0, -3.0, -4.0, -6.0])


def pack_weight(w, fmt):
    k, n = w.shape
    w = f64(bf(w)).reshape(k // 32, 32, n)
    amax = np.abs(w).max(1)
    if fmt == "e4m3":
        byte = np.frexp(amax)[1] - 1 + 127 - 7
    else:
        mant, ex = np.frexp(amax / 6.0)
        byte = np.where(mant > 0.5, ex, ex - 1) + 127
    byte = np.clip(np.where(amax > 0, byte, 1), 1, 254)
    scaled = (w * np.exp2(127.0 - byte)[:, None, :]).reshape(k, n).astype(np.float32)
    by_word = np.ascontiguousarray(scaled.reshape(k // 512, 128, 4, n).transpose(0, 1, 3, 2))
    if fmt == "e4m3":
        words = by_word.astype(ml_dtypes.float8_e4m3fn).view(np.uint8)
    else:
        c = by_word.astype(ml_dtypes.float4_e2m1fn).view(np.uint8) & 0xF
        words = c[..., 0::2] | (c[..., 1::2] << 4)
    return np.ascontiguousarray(words), np.ascontiguousarray(byte.astype(np.uint8).reshape(k // 512, 16, n))


def unpack_weight(words, scales, fmt):
    g, p, n, _ = words.shape
    if fmt == "e4m3":
        vals = np.ascontiguousarray(words).view(ml_dtypes.float8_e4m3fn).astype(np.float64)
    else:
        nib = np.empty((g, p, n, 4), np.uint8)
        nib[..., 0::2] = words & 0xF
        nib[..., 1::2] = words >> 4
        vals = E2M1[nib]
    vals = vals * np.repeat(np.exp2(scales.astype(np.float64) - 127.0), 8, axis=1)[..., None]
    return vals.transpose(0, 1, 3, 2).reshape(g * 512, n)
def pack4(w):
    words, scales = pack_weight(w, "e2m1")
    return words.reshape(words.shape[0], 128, -1), scales


def unpack4(words, scales):
    return unpack_weight(words.reshape(words.shape[0], 128, -1, 2), scales, "e2m1")


def planes(Y):
    n, m = Y.shape
    b = f64(bf(Y)).reshape(n // 32, 32, m)
    amax = np.abs(b).max(1)
    byte = np.clip(np.where(amax > 0, np.frexp(amax)[1] - 1 + 127 - 7, 1), 1, 254)
    codes = (b * np.exp2(127.0 - byte)[:, None, :]).reshape(n, m).astype(np.float32).astype(ml_dtypes.float8_e4m3fn).view(np.uint8)
    words = codes.reshape(n // 512, 128, 4, m).transpose(0, 1, 3, 2)
    return np.ascontiguousarray(words), np.ascontiguousarray(byte.astype(np.uint8).reshape(n // 512, 16, m))


L, D, N = 768, 1536, 1024

def setup_inputs():
    s = mx_kscale(D)[:, None]
    alloc = bf(np.random.randn(D, L) * s)
    amp = bf(np.random.randn(D, N) / np.sqrt(D) / s)
    turn = bf(0.8 * np.random.randn(D, N) / np.sqrt(D) / s)
    spread = np.exp(0.8 * np.random.randn(N))
    volt = bf(np.random.randn(D, N) * spread / np.sqrt(D) / s)
    alloc_words, alloc_scales = pack_weight(f64(alloc), "e4m3")
    amp_words, amp_scales = pack_weight(f64(amp), "e4m3")
    turn_words, turn_scales = pack4(f64(turn))
    return {"alloc_words": alloc_words, "alloc_scales": alloc_scales,
            "amp_words": amp_words, "amp_scales": amp_scales,
            "turn_words": turn_words, "turn_scales": turn_scales, "volt": volt}

def reference(alloc_words, alloc_scales, amp_words, amp_scales, turn_words, turn_scales, volt):
    A = unpack_weight(alloc_words, alloc_scales, "e4m3")
    H = unpack_weight(amp_words, amp_scales, "e4m3")
    C = unpack4(turn_words, turn_scales)
    V = mxq(f64(volt), 0, "e4m3")
    a = A.T @ H
    c = A.T @ C
    v = A.T @ V
    y = v / (1.0 + np.exp(-(a * a - c)))
    Y = y.T
    words, scales = planes(Y)
    return y, words, scales

@@ -1,0 +1,261 @@
+from contextlib import ExitStack
+
+import concourse.mybir as mybir
+from concourse.masks import make_identity
+
+L, D, N = 768, 1536, 1024
+FLOPS = 3 * 2 * L * D * N
+
+F32 = mybir.dt.float32
+BF16 = mybir.dt.bfloat16
+I32 = mybir.dt.int32
+U32 = mybir.dt.uint32
+U8 = mybir.dt.uint8
+FP8X4 = mybir.dt.float8_e4m3fn_x4
+FP4X4 = mybir.dt.float4_e2m1fn_x4
+ACT = mybir.ActivationFunctionType
+ALU = mybir.AluOpType
+
+P = 128
+PACK = 4
+G = D // (P * PACK)
+W = 512
+NH = N // W
+LT = L // P
+BANKS = 8
+H_ROW = 4
+
+PE_ORDER = "c00 c01 c02 c03 c04 c05 a10 a11 a12 a13 a14 a15 v00 c10 v01 c11 v02 c12 v03 c13 v04 c14 t00 t02 v05 c15 v10 v11 v12 v13 t04 t10 v14 v15 t12 t14 t15"
+ACT_ORDER = "sq00 sq01 sq02 sq03 sq04 sq05 il01 sg00 sg01 sq10 sg02 sq11 sg03 sq12 sg04 sq13 sg05 sq14 sq15 il12 cast00 cast01 sg10 cast02 sg11 cast03 sg12 sg13 cp00 cp02 cast04 sg14 cast05 sg15 cast10 cast12 cp04 cp10 cast14 cp12 cp14 cp15 os12 os13"
+DVE_ORDER = "sub00 il00 sub01 sub02 q00 sub03 sub04 il02 q01 sub05 q02 il10 il11 q10 mul00 q11 sub10 mul01 sub11 mul02 sub12 q12 mul03 sub13 mul04 sub14 mul05 qy00 sub15 qy02 mul10 mul11 mul12 cast11 mul13 cast13 qy04 mul14 qy10 mulb15 mul15 qy12 qy14 qy15"
+SP_ORDER = "oy00 oy01 oy02 oy03 oy04 oy05 oy10 oy11 oy12 oy13 ow00 os00 os01 os02 os03 oy14 oy15 ow10 ow14 os10 os11"
+TURNS = {(0, 0): 2, (0, 2): 2, (0, 4): 2, (1, 0): 2, (1, 2): 2, (1, 4): 1, (1, 5): 1}
+
+
+def tile_rf_combined_rectifier_saturation_k3_kernel(
+    tc, alloc_words, alloc_scales, amp_words, amp_scales, turn_words, turn_scales, volt, out_0, out_1, out_2
+):
+    nc = tc.nc
+    with ExitStack() as ctx:
+        keep = ctx.enter_context(tc.tile_pool(name="keep", bufs=1))
+        ring = ctx.enter_context(tc.tile_pool(name="ring", bufs=3))
+        psum = ctx.enter_context(tc.psum_pool(name="psum", bufs=1))
+        ctx.enter_context(tc.manual_schedule())
+
+        banks = [psum.tile([P, W], F32, name="bank%d" % i) for i in range(BANKS)]
+        ah_scales = keep.tile([P, G * N], U8, align_bytes=64)
+        c_scales = keep.tile([P, G * N], U8, align_bytes=64)
+        a_words = [keep.tile([P, L], U32, name="a_words%d" % g, align_bytes=64) for g in range(G)]
+        h_words = {(n, g): keep.tile([P, W], U32, name="h_words%d%d" % (n, g), align_bytes=64) for n in range(NH) for g in range(G)}
+        c_words = [keep.tile([P, G, 2 * W], U8, name="c_words%d" % n, align_bytes=64) for n in range(NH)]
+        v_raw = {(n, g): keep.tile([P, PACK, W], BF16, name="v_raw%d%d" % (n, g), align_bytes=64) for n in range(NH) for g in range(G)}
+        v_words = {(n, g): keep.tile([P, W], U32, name="v_words%d%d" % (n, g), align_bytes=64) for n in range(NH) for g in range(G)}
+        v_scales = {(n, g): keep.tile([P, W], U8, name="v_scales%d%d" % (n, g), align_bytes=64) for n in range(NH) for g in range(G)}
+        y_words = [keep.tile([P, L], U32, name="y_words%d" % n, align_bytes=64) for n in range(NH)]
+        y_scales = [keep.tile([P, L], U8, name="y_scales%d" % n, align_bytes=64) for n in range(NH)]
+        ident = keep.tile([P, P], F32, align_bytes=64)
+        warm = keep.tile([P, 8], F32)
+
+        def load_scales(engine, plane, first_row, src, r):
+            width = src.shape[2]
+            rows = src.bitcast(I32).rearrange("g (q r) n -> r q g n", r=4)[r]
+            dst = plane[first_row + r : P : 32, 0 : G * width].bitcast(I32).rearrange("q (g n) -> q g n", g=G)
+            engine.dma_start(out=dst, in_=rows)
+
+        def load_a(engine, g):
+            engine.dma_start(out=a_words[g][:].bitcast(I32), in_=alloc_words[g].rearrange("p m t -> p (m t)").bitcast(I32))
+
+        def load_h(engine, n, g):
+            src = amp_words[g].rearrange("p m t -> p (m t)")[:, n * W * 4 : (n + 1) * W * 4]
+            engine.dma_start(out=h_words[n, g][:].bitcast(I32), in_=src.bitcast(I32))
+
+        def load_c(n):
+            src = turn_words[:, :, n * W * 2 : (n + 1) * W * 2].bitcast(I32).rearrange("g p b -> p g b")
+            nc.sync.dma_start(out=c_words[n][:].bitcast(I32), in_=src)
+
+        def load_v(n, g):
+            src = volt[g * 512 : (g + 1) * 512, n * W : (n + 1) * W].rearrange("(p j) w -> p j w", j=PACK)
+            nc.sync.dma_start(out=v_raw[n, g][:], in_=src)
+
+        nc.vector.memset(ah_scales[:].bitcast(I32), 0)
+        nc.vector.memset(c_scales[:].bitcast(I32), 0)
+        nc.vector.memset(warm[:, 0:1], 0.0)
+        load_h(nc.gpsimd, 0, 0)
+        load_a(nc.gpsimd, 0)
+        for r in range(4):
+            load_scales(nc.sync, ah_scales, 0, alloc_scales, r)
+            load_scales(nc.scalar, ah_scales, H_ROW, amp_scales, r)
+        for r in range(4):
+            load_scales(nc.sync, c_scales, 0, turn_scales, r)
+        nc.scalar.activation(out=warm[:, 1:2], in_=warm[:, 0:1], func=ACT.Sigmoid)
+        make_identity(nc, ident[:])
+        for g in (1, 2):
+            load_a(nc.sync, g)
+            load_h(nc.sync, 0, g)
+        load_c(0)
+        load_v(0, 0)
+        load_v(0, 1)
+        for g in range(G):
+            load_h(nc.sync, 1, g)
+        load_v(0, 2)
+        load_c(1)
+        for g in range(G):
+            load_v(1, g)
+
+        held = {}
+
+        def mx_pass(kind, n, l, g):
+            if kind == "a":
+                rhs = h_words[n, g][:].bitcast(FP8X4)
+                rhs_scale = ah_scales[H_ROW:P, g * N + n * W : g * N + (n + 1) * W]
+            elif kind == "c":
+                rhs = c_words[n][:, g, :].bitcast(FP4X4)
+                rhs_scale = c_scales[:, g * N + n * W : g * N + (n + 1) * W]
+            else:
+                rhs = v_words[n, g][:].bitcast(FP8X4)
+                rhs_scale = v_scales[n, g][:]
+            nc.tensor.matmul_mx(
+                out=held[kind, n, l][:],
+                lhsT=a_words[g][:, l * P : (l + 1) * P].bitcast(FP8X4),
+                lhsT_scale=ah_scales[:, g * L + l * P : g * L + (l + 1) * P],
+                rhs=rhs,
+                rhs_scale=rhs_scale,
+                start=(g == 0),
+                stop=(g == G - 1),
+            )
+
+        def copy_on(engine, out, in_):
+            if engine == "scalar":
+                nc.scalar.copy(out=out, in_=in_)
+            else:
+                nc.vector.tensor_copy(out=out, in_=in_)
+
+        def pair_order(ap):
+            return ap.rearrange("m (p u e) -> m u p e", u=2, e=2)
+
+        def emit(engine, kind, n, l):
+            if kind in ("a", "c", "v"):
+                for g in range(G):
+                    mx_pass(kind, n, l, g)
+            elif kind == "sq":
+                sq = keep.tile([P, W], F32, name="sq%d" % l)
+                held["sq", n, l] = sq
+                nc.scalar.activation(out=sq[:], in_=held["a", n, l][:], func=ACT.Square)
+            elif kind == "sub":
+                z = ring.tile([P, W], F32, name="z", bufs=6)
+                held["sub", n, l] = z
+                nc.vector.tensor_tensor(out=z[:], in0=held["sq", n, l][:], in1=held["c", n, l][:], op=ALU.subtract)
+            elif kind == "sg":
+                s = keep.tile([P, W], F32, name="s%d%d" % (n, l))
+                held["sg", n, l] = s
+                nc.scalar.activation(out=s[:], in_=held["sub", n, l][:], func=ACT.Sigmoid)
+            elif kind == "mul":
+                y = keep.tile([P, W], F32, name="y%d%d" % (n, l))
+                held["mul", n, l] = y
+                nc.vector.tensor_tensor(out=y[:], in0=held["sg", n, l][:], in1=held["v", n, l][:], op=ALU.mult)
+            elif kind == "cast":
+                yb = ring.tile([P, 2, P, 2], BF16, name="yb", bufs=8, align_bytes=64)
+                held["cast", n, l] = yb
+                copy_on(engine, yb[:], pair_order(held["mul", n, l][:]))
+            elif kind == "mulb":
+                yb = ring.tile([P, 2, P, 2], BF16, name="yb", bufs=8, align_bytes=64)
+                held["cast", n, l] = yb
+                nc.vector.tensor_tensor(
+                    out=yb[:], in0=pair_order(held["sg", n, l][:]), in1=pair_order(held["v", n, l][:]), op=ALU.mult
+                )
+            elif kind == "t":
+                for j in range(TURNS[n, l]):
+                    words = held["cast", n, l + j][:].rearrange("m u p e -> m (u p e)").bitcast(F32)
+                    for u in range(2):
+                        col = (2 * j + u) * P
+                        nc.tensor.transpose(held["t", n, l][:, col : col + P], words[:, u * P : (u + 1) * P], ident[:])
+            elif kind == "cp":
+                count = TURNS[n, l]
+                yt = ring.tile([P, 2 * P, PACK], BF16, name="yt", bufs=4, align_bytes=64)
+                held["cp", n, l] = yt
+                dst = yt[:, 0 : count * P, :].rearrange("p m t -> p (m t)").bitcast(F32)
+                nc.scalar.copy(
+                    out=dst.rearrange("p (j m u) -> p j m u", j=count, u=2),
+                    in_=held["t", n, l][:, 0 : count * 2 * P].rearrange("p (j u m) -> p j m u", j=count, u=2),
+                )
+            elif kind == "qy":
+                cols = slice(l * P, (l + TURNS[n, l]) * P)
+                nc.vector.quantize_mx(
+                    out=y_words[n][:, cols].bitcast(FP8X4),
+                    scales=y_scales[n][:, cols],
+                    in_=held["cp", n, l][:, 0 : TURNS[n, l] * P, :].rearrange("p m t -> p (m t)"),
+                )
+            elif kind == "il":
+                grouped = ring.tile([P, W, PACK], BF16, name="grouped", bufs=3, align_bytes=64)
+                held["il", n, l] = grouped
+                copy_on(
+                    engine,
+                    grouped[:].rearrange("p (c i) t -> p c t i", i=4),
+                    v_raw[n, l][:].rearrange("p t (c i) -> p c t i", i=4),
+                )
+            elif kind == "q":
+                nc.vector.quantize_mx(
+                    out=v_words[n, l][:].bitcast(FP8X4),
+                    scales=v_scales[n, l][:],
+                    in_=held["il", n, l][:].rearrange("p c t -> p (c t)"),
+                )
+            elif kind == "oy":
+                nc.sync.dma_start(out=out_0[l * P : (l + 1) * P, n * W : (n + 1) * W], in_=held["mul", n, l][:])
+            elif kind == "ow":
+                cols = slice(l * P, L if (n == 0 or l > 0) else 4 * P)
+                dst = out_1[n].rearrange("p m t -> p (m t)").bitcast(I32)
+                nc.sync.dma_start(out=dst[:, cols], in_=y_words[n][:, cols].bitcast(I32))
+            else:
+                (nc.scalar if engine == "scalar" else nc.sync).dma_start(
+                    out=out_2[n, 4 * l : 4 * l + 4, :].bitcast(I32), in_=y_scales[n][32 * l : 32 * l + 4, :].bitcast(I32)
+                )
+
+        def needs(kind, n, l):
+            if kind == "v":
+                return [("q", n, g) for g in range(G)]
+            if kind == "t":
+                return [("cast", n, l + j) for j in range(TURNS[n, l])]
+            if kind == "ow":
+                return [("qy", n, 4 if n == 0 else (2 if l == 0 else 5))]
+            if kind == "os":
+                return [("qy", n, 4 if n == 0 else 5)]
+            table = {
+                "sq": ["a"], "sub": ["sq", "c"], "sg": ["sub"], "mul": ["sg", "v"], "mulb": ["sg", "v"], "cast": ["mul"],
+                "cp": ["t"], "qy": ["cp"], "q": ["il"], "oy": ["mul"],
+            }
+            return [(k, n, l) for k in table.get(kind, [])]
+
+        empties = {"a": "sq", "c": "sub", "v": "mul", "t": "cp"}
+
+        used = []
+        for l in range(LT):
+            held["a", 0, l] = banks[l]
+            used.append(("a", 0, l))
+        for g in range(G):
+            for l in range(LT):
+                mx_pass("a", 0, l, g)
+        done = set(used)
+
+        queues = [
+            (engine, [(w[:-2], int(w[-2]), int(w[-1])) for w in order.split()])
+            for engine, order in (("tensor", PE_ORDER), ("scalar", ACT_ORDER), ("vector", DVE_ORDER), ("sync", SP_ORDER))
+        ]
+        while any(queue for engine, queue in queues):
+            moved = False
+            for engine, queue in queues:
+                while queue:
+                    kind, n, l = queue[0]
+                    wanted = needs(kind, n, l)
+                    if engine == "tensor" and len(used) >= BANKS:
+                        old = used[len(used) - BANKS]
+                        wanted = wanted + [(empties[old[0]], old[1], old[2])]
+                    if not all(w in done for w in wanted):
+                        break
+                    if engine == "tensor":
+                        held[kind, n, l] = banks[len(used) % BANKS]
+                        used.append((kind, n, l))
+                    emit(engine, kind, n, l)
+                    done.add(("cast" if kind == "mulb" else kind, n, l))
+                    queue.pop(0)
+                    moved = True
+            assert moved

@@ -80,18 +80,31 @@ def tile_rf_combined_rectifier_saturation_k3_kernel(
         nc.vector.memset(ah_scales[:].bitcast(I32), 0)
         nc.vector.memset(c_scales[:].bitcast(I32), 0)
         nc.vector.memset(warm[:, 0:1], 0.0)
-        load_h(nc.gpsimd, 0, 0)
-        load_a(nc.gpsimd, 0)
+        load_h(nc.sync, 0, 0)
         for r in range(4):
             load_scales(nc.sync, ah_scales, 0, alloc_scales, r)
-            load_scales(nc.scalar, ah_scales, H_ROW, amp_scales, r)
-        for r in range(4):
-            load_scales(nc.sync, c_scales, 0, turn_scales, r)
+        for r in range(2):
+            load_scales(nc.sync, ah_scales, H_ROW, amp_scales, r)
+        load_a(nc.sync, 0)
+        for r in range(2, 4):
+            load_scales(nc.sync, ah_scales, H_ROW, amp_scales, r)
         nc.scalar.activation(out=warm[:, 1:2], in_=warm[:, 0:1], func=ACT.Sigmoid)
         make_identity(nc, ident[:])
+        for i in range(4):
+            nc.tensor.matmul_mx(
+                out=banks[BANKS - 1][:],
+                lhsT=h_words[0, 0][:, 0:P].bitcast(FP8X4),
+                lhsT_scale=c_scales[:, 0:P],
+                rhs=h_words[0, 0][:].bitcast(FP8X4),
+                rhs_scale=c_scales[:, 0:W],
+                start=True,
+                stop=True,
+            )
         for g in (1, 2):
             load_a(nc.sync, g)
             load_h(nc.sync, 0, g)
+        for r in range(4):
+            load_scales(nc.sync, c_scales, 0, turn_scales, r)
         load_c(0)
         load_v(0, 0)
         load_v(0, 1)

@@ -25,9 +25,9 @@ LT = L // P
 BANKS = 8
 H_ROW = 4
 
-PE_ORDER = "c00 c01 c02 c03 c04 c05 a10 a11 a12 a13 a14 a15 v00 c10 v01 c11 v02 c12 v03 c13 v04 c14 t00 t02 v05 c15 v10 v11 v12 v13 t04 t10 v14 v15 t12 t14 t15"
-ACT_ORDER = "sq00 sq01 sq02 sq03 sq04 sq05 il01 sg00 sg01 sq10 sg02 sq11 sg03 sq12 sg04 sq13 sg05 sq14 sq15 il12 cast00 cast01 sg10 cast02 sg11 cast03 sg12 sg13 cp00 cp02 cast04 sg14 cast05 sg15 cast10 cast12 cp04 cp10 cast14 cp12 cp14 cp15 os12 os13"
-DVE_ORDER = "sub00 il00 sub01 sub02 q00 sub03 sub04 il02 q01 sub05 q02 il10 il11 q10 mul00 q11 sub10 mul01 sub11 mul02 sub12 q12 mul03 sub13 mul04 sub14 mul05 qy00 sub15 qy02 mul10 mul11 mul12 cast11 mul13 cast13 qy04 mul14 qy10 mulb15 mul15 qy12 qy14 qy15"
+PE_ORDER = "c00 c01 c02 c03 c04 c05 a10 a11 a12 a13 a14 a15 v00 c10 v01 c11 v02 c12 v03 c13 v04 c14 v05 c15 v10 v11 t00 t02 t04 v12 v13 v14 v15 t10 t12 t14 t15"
+ACT_ORDER = "sq00 sq01 sq02 sq03 sq04 sq05 il01 sg00 sg01 sq10 sg02 sq11 sg03 sq12 sg04 sq13 sg05 sq14 sq15 il12 cast00 cast01 sg10 cast02 sg11 cast03 sg12 sg13 cast04 sg14 cast05 sg15 cast10 cp00 cp02 cp04 cast12 cast13 cp10 cp12 cp15 os12 os13"
+DVE_ORDER = "sub00 il00 sub01 sub02 q00 sub03 sub04 il02 q01 sub05 q02 il10 il11 q10 mul00 q11 sub10 mul01 sub11 mul02 sub12 q12 mul03 sub13 mul04 sub14 mul05 sub15 mul10 mul11 cast11 qy00 mul12 qy02 mul13 qy04 mul14 cast14 mulb15 mul15 qy10 cp14 qy12 qy14 qy15"
 SP_ORDER = "oy00 oy01 oy02 oy03 oy04 oy05 oy10 oy11 oy12 oy13 ow00 os00 os01 os02 os03 oy14 oy15 ow10 ow14 os10 os11"
 TURNS = {(0, 0): 2, (0, 2): 2, (0, 4): 2, (1, 0): 2, (1, 2): 2, (1, 4): 1, (1, 5): 1}
 
@@ -167,11 +167,11 @@ def tile_rf_combined_rectifier_saturation_k3_kernel(
                 held["mul", n, l] = y
                 nc.vector.tensor_tensor(out=y[:], in0=held["sg", n, l][:], in1=held["v", n, l][:], op=ALU.mult)
             elif kind == "cast":
-                yb = ring.tile([P, 2, P, 2], BF16, name="yb", bufs=8, align_bytes=64)
+                yb = ring.tile([P, 2, P, 2], BF16, name="yb", bufs=12, align_bytes=64)
                 held["cast", n, l] = yb
                 copy_on(engine, yb[:], pair_order(held["mul", n, l][:]))
             elif kind == "mulb":
-                yb = ring.tile([P, 2, P, 2], BF16, name="yb", bufs=8, align_bytes=64)
+                yb = ring.tile([P, 2, P, 2], BF16, name="yb", bufs=12, align_bytes=64)
                 held["cast", n, l] = yb
                 nc.vector.tensor_tensor(
                     out=yb[:], in0=pair_order(held["sg", n, l][:]), in1=pair_order(held["v", n, l][:]), op=ALU.mult
@@ -187,9 +187,10 @@ def tile_rf_combined_rectifier_saturation_k3_kernel(
                 yt = ring.tile([P, 2 * P, PACK], BF16, name="yt", bufs=4, align_bytes=64)
                 held["cp", n, l] = yt
                 dst = yt[:, 0 : count * P, :].rearrange("p m t -> p (m t)").bitcast(F32)
-                nc.scalar.copy(
-                    out=dst.rearrange("p (j m u) -> p j m u", j=count, u=2),
-                    in_=held["t", n, l][:, 0 : count * 2 * P].rearrange("p (j u m) -> p j m u", j=count, u=2),
+                copy_on(
+                    engine,
+                    dst.rearrange("p (j m u) -> p j m u", j=count, u=2),
+                    held["t", n, l][:, 0 : count * 2 * P].rearrange("p (j u m) -> p j m u", j=count, u=2),
                 )
             elif kind == "qy":
                 cols = slice(l * P, (l + TURNS[n, l]) * P)

from contextlib import ExitStack

import concourse.mybir as mybir
from concourse.masks import make_identity

L, D, N = 768, 1536, 1024
FLOPS = 3 * 2 * L * D * N

F32 = mybir.dt.float32
BF16 = mybir.dt.bfloat16
I32 = mybir.dt.int32
U32 = mybir.dt.uint32
U8 = mybir.dt.uint8
FP8X4 = mybir.dt.float8_e4m3fn_x4
FP4X4 = mybir.dt.float4_e2m1fn_x4
ACT = mybir.ActivationFunctionType
ALU = mybir.AluOpType

P = 128
PACK = 4
G = D // (P * PACK)
W = 512
NH = N // W
LT = L // P
BANKS = 8
H_ROW = 4

PE_ORDER = "c00 c01 c02 c03 c04 c05 a10 a11 a12 a13 a14 a15 v00 c10 v01 c11 v02 c12 v03 c13 v04 c14 v05 c15 v10 v11 t00 t02 t04 v12 v13 v14 v15 t10 t12 t14 t15"
ACT_ORDER = "sq00 sq01 sq02 sq03 sq04 sq05 il01 sg00 sg01 sq10 sg02 sq11 sg03 sq12 sg04 sq13 sg05 sq14 sq15 il12 cast00 cast01 sg10 cast02 sg11 cast03 sg12 sg13 cast04 sg14 cast05 sg15 cast10 cp00 cp02 cp04 cast12 cast13 cp10 cp12 cp15 os12 os13"
DVE_ORDER = "sub00 il00 sub01 sub02 q00 sub03 sub04 il02 q01 sub05 q02 il10 il11 q10 mul00 q11 sub10 mul01 sub11 mul02 sub12 q12 mul03 sub13 mul04 sub14 mul05 sub15 mul10 mul11 cast11 qy00 mul12 qy02 mul13 qy04 mul14 cast14 mulb15 mul15 qy10 cp14 qy12 qy14 qy15"
SP_ORDER = "oy00 oy01 oy02 oy03 oy04 oy05 oy10 oy11 oy12 oy13 ow00 os00 os01 os02 os03 oy14 oy15 ow10 ow14 os10 os11"
TURNS = {(0, 0): 2, (0, 2): 2, (0, 4): 2, (1, 0): 2, (1, 2): 2, (1, 4): 1, (1, 5): 1}


def tile_rf_combined_rectifier_saturation_k3_kernel(
    tc, alloc_words, alloc_scales, amp_words, amp_scales, turn_words, turn_scales, volt, out_0, out_1, out_2
):
    nc = tc.nc
    with ExitStack() as ctx:
        keep = ctx.enter_context(tc.tile_pool(name="keep", bufs=1))
        ring = ctx.enter_context(tc.tile_pool(name="ring", bufs=3))
        psum = ctx.enter_context(tc.psum_pool(name="psum", bufs=1))
        ctx.enter_context(tc.manual_schedule())

        banks = [psum.tile([P, W], F32, name="bank%d" % i) for i in range(BANKS)]
        ah_scales = keep.tile([P, G * N], U8, align_bytes=64)
        c_scales = keep.tile([P, G * N], U8, align_bytes=64)
        a_words = [keep.tile([P, L], U32, name="a_words%d" % g, align_bytes=64) for g in range(G)]
        h_words = {(n, g): keep.tile([P, W], U32, name="h_words%d%d" % (n, g), align_bytes=64) for n in range(NH) for g in range(G)}
        c_words = [keep.tile([P, G, 2 * W], U8, name="c_words%d" % n, align_bytes=64) for n in range(NH)]
        v_raw = {(n, g): keep.tile([P, PACK, W], BF16, name="v_raw%d%d" % (n, g), align_bytes=64) for n in range(NH) for g in range(G)}
        v_words = {(n, g): keep.tile([P, W], U32, name="v_words%d%d" % (n, g), align_bytes=64) for n in range(NH) for g in range(G)}
        v_scales = {(n, g): keep.tile([P, W], U8, name="v_scales%d%d" % (n, g), align_bytes=64) for n in range(NH) for g in range(G)}
        y_words = [keep.tile([P, L], U32, name="y_words%d" % n, align_bytes=64) for n in range(NH)]
        y_scales = [keep.tile([P, L], U8, name="y_scales%d" % n, align_bytes=64) for n in range(NH)]
        ident = keep.tile([P, P], F32, align_bytes=64)
        warm = keep.tile([P, 8], F32)

        def load_scales(engine, plane, first_row, src, r):
            width = src.shape[2]
            rows = src.bitcast(I32).rearrange("g (q r) n -> r q g n", r=4)[r]
            dst = plane[first_row + r : P : 32, 0 : G * width].bitcast(I32).rearrange("q (g n) -> q g n", g=G)
            engine.dma_start(out=dst, in_=rows)

        def load_a(engine, g):
            engine.dma_start(out=a_words[g][:].bitcast(I32), in_=alloc_words[g].rearrange("p m t -> p (m t)").bitcast(I32))

        def load_h(engine, n, g):
            src = amp_words[g].rearrange("p m t -> p (m t)")[:, n * W * 4 : (n + 1) * W * 4]
            engine.dma_start(out=h_words[n, g][:].bitcast(I32), in_=src.bitcast(I32))

        def load_c(n):
            src = turn_words[:, :, n * W * 2 : (n + 1) * W * 2].bitcast(I32).rearrange("g p b -> p g b")
            nc.sync.dma_start(out=c_words[n][:].bitcast(I32), in_=src)

        def load_v(n, g):
            src = volt[g * 512 : (g + 1) * 512, n * W : (n + 1) * W].rearrange("(p j) w -> p j w", j=PACK)
            nc.sync.dma_start(out=v_raw[n, g][:], in_=src)

        nc.vector.memset(ah_scales[:].bitcast(I32), 0)
        nc.vector.memset(c_scales[:].bitcast(I32), 0)
        nc.vector.memset(warm[:, 0:1], 0.0)
        load_h(nc.sync, 0, 0)
        for r in range(4):
            load_scales(nc.sync, ah_scales, 0, alloc_scales, r)
        for r in range(2):
            load_scales(nc.sync, ah_scales, H_ROW, amp_scales, r)
        load_a(nc.sync, 0)
        for r in range(2, 4):
            load_scales(nc.sync, ah_scales, H_ROW, amp_scales, r)
        nc.scalar.activation(out=warm[:, 1:2], in_=warm[:, 0:1], func=ACT.Sigmoid)
        make_identity(nc, ident[:])
        for i in range(4):
            nc.tensor.matmul_mx(
                out=banks[BANKS - 1][:],
                lhsT=h_words[0, 0][:, 0:P].bitcast(FP8X4),
                lhsT_scale=c_scales[:, 0:P],
                rhs=h_words[0, 0][:].bitcast(FP8X4),
                rhs_scale=c_scales[:, 0:W],
                start=True,
                stop=True,
            )
        for g in (1, 2):
            load_a(nc.sync, g)
            load_h(nc.sync, 0, g)
        for r in range(4):
            load_scales(nc.sync, c_scales, 0, turn_scales, r)
        load_c(0)
        load_v(0, 0)
        load_v(0, 1)
        for g in range(G):
            load_h(nc.sync, 1, g)
        load_v(0, 2)
        load_c(1)
        for g in range(G):
            load_v(1, g)

        held = {}

        def mx_pass(kind, n, l, g):
            if kind == "a":
                rhs = h_words[n, g][:].bitcast(FP8X4)
                rhs_scale = ah_scales[H_ROW:P, g * N + n * W : g * N + (n + 1) * W]
            elif kind == "c":
                rhs = c_words[n][:, g, :].bitcast(FP4X4)
                rhs_scale = c_scales[:, g * N + n * W : g * N + (n + 1) * W]
            else:
                rhs = v_words[n, g][:].bitcast(FP8X4)
                rhs_scale = v_scales[n, g][:]
            nc.tensor.matmul_mx(
                out=held[kind, n, l][:],
                lhsT=a_words[g][:, l * P : (l + 1) * P].bitcast(FP8X4),
                lhsT_scale=ah_scales[:, g * L + l * P : g * L + (l + 1) * P],
                rhs=rhs,
                rhs_scale=rhs_scale,
                start=(g == 0),
                stop=(g == G - 1),
            )

        def copy_on(engine, out, in_):
            if engine == "scalar":
                nc.scalar.copy(out=out, in_=in_)
            else:
                nc.vector.tensor_copy(out=out, in_=in_)

        def pair_order(ap):
            return ap.rearrange("m (p u e) -> m u p e", u=2, e=2)

        def emit(engine, kind, n, l):
            if kind in ("a", "c", "v"):
                for g in range(G):
                    mx_pass(kind, n, l, g)
            elif kind == "sq":
                sq = keep.tile([P, W], F32, name="sq%d" % l)
                held["sq", n, l] = sq
                nc.scalar.activation(out=sq[:], in_=held["a", n, l][:], func=ACT.Square)
            elif kind == "sub":
                z = ring.tile([P, W], F32, name="z", bufs=6)
                held["sub", n, l] = z
                nc.vector.tensor_tensor(out=z[:], in0=held["sq", n, l][:], in1=held["c", n, l][:], op=ALU.subtract)
            elif kind == "sg":
                s = keep.tile([P, W], F32, name="s%d%d" % (n, l))
                held["sg", n, l] = s
                nc.scalar.activation(out=s[:], in_=held["sub", n, l][:], func=ACT.Sigmoid)
            elif kind == "mul":
                y = keep.tile([P, W], F32, name="y%d%d" % (n, l))
                held["mul", n, l] = y
                nc.vector.tensor_tensor(out=y[:], in0=held["sg", n, l][:], in1=held["v", n, l][:], op=ALU.mult)
            elif kind == "cast":
                yb = ring.tile([P, 2, P, 2], BF16, name="yb", bufs=12, align_bytes=64)
                held["cast", n, l] = yb
                copy_on(engine, yb[:], pair_order(held["mul", n, l][:]))
            elif kind == "mulb":
                yb = ring.tile([P, 2, P, 2], BF16, name="yb", bufs=12, align_bytes=64)
                held["cast", n, l] = yb
                nc.vector.tensor_tensor(
                    out=yb[:], in0=pair_order(held["sg", n, l][:]), in1=pair_order(held["v", n, l][:]), op=ALU.mult
                )
            elif kind == "t":
                for j in range(TURNS[n, l]):
                    words = held["cast", n, l + j][:].rearrange("m u p e -> m (u p e)").bitcast(F32)
                    for u in range(2):
                        col = (2 * j + u) * P
                        nc.tensor.transpose(held["t", n, l][:, col : col + P], words[:, u * P : (u + 1) * P], ident[:])
            elif kind == "cp":
                count = TURNS[n, l]
                yt = ring.tile([P, 2 * P, PACK], BF16, name="yt", bufs=4, align_bytes=64)
                held["cp", n, l] = yt
                dst = yt[:, 0 : count * P, :].rearrange("p m t -> p (m t)").bitcast(F32)
                copy_on(
                    engine,
                    dst.rearrange("p (j m u) -> p j m u", j=count, u=2),
                    held["t", n, l][:, 0 : count * 2 * P].rearrange("p (j u m) -> p j m u", j=count, u=2),
                )
            elif kind == "qy":
                cols = slice(l * P, (l + TURNS[n, l]) * P)
                nc.vector.quantize_mx(
                    out=y_words[n][:, cols].bitcast(FP8X4),
                    scales=y_scales[n][:, cols],
                    in_=held["cp", n, l][:, 0 : TURNS[n, l] * P, :].rearrange("p m t -> p (m t)"),
                )
            elif kind == "il":
                grouped = ring.tile([P, W, PACK], BF16, name="grouped", bufs=3, align_bytes=64)
                held["il", n, l] = grouped
                copy_on(
                    engine,
                    grouped[:].rearrange("p (c i) t -> p c t i", i=4),
                    v_raw[n, l][:].rearrange("p t (c i) -> p c t i", i=4),
                )
            elif kind == "q":
                nc.vector.quantize_mx(
                    out=v_words[n, l][:].bitcast(FP8X4),
                    scales=v_scales[n, l][:],
                    in_=held["il", n, l][:].rearrange("p c t -> p (c t)"),
                )
            elif kind == "oy":
                nc.sync.dma_start(out=out_0[l * P : (l + 1) * P, n * W : (n + 1) * W], in_=held["mul", n, l][:])
            elif kind == "ow":
                cols = slice(l * P, L if (n == 0 or l > 0) else 4 * P)
                dst = out_1[n].rearrange("p m t -> p (m t)").bitcast(I32)
                nc.sync.dma_start(out=dst[:, cols], in_=y_words[n][:, cols].bitcast(I32))
            else:
                (nc.scalar if engine == "scalar" else nc.sync).dma_start(
                    out=out_2[n, 4 * l : 4 * l + 4, :].bitcast(I32), in_=y_scales[n][32 * l : 32 * l + 4, :].bitcast(I32)
                )

        def needs(kind, n, l):
            if kind == "v":
                return [("q", n, g) for g in range(G)]
            if kind == "t":
                return [("cast", n, l + j) for j in range(TURNS[n, l])]
            if kind == "ow":
                return [("qy", n, 4 if n == 0 else (2 if l == 0 else 5))]
            if kind == "os":
                return [("qy", n, 4 if n == 0 else 5)]
            table = {
                "sq": ["a"], "sub": ["sq", "c"], "sg": ["sub"], "mul": ["sg", "v"], "mulb": ["sg", "v"], "cast": ["mul"],
                "cp": ["t"], "qy": ["cp"], "q": ["il"], "oy": ["mul"],
            }
            return [(k, n, l) for k in table.get(kind, [])]

        empties = {"a": "sq", "c": "sub", "v": "mul", "t": "cp"}

        used = []
        for l in range(LT):
            held["a", 0, l] = banks[l]
            used.append(("a", 0, l))
        for g in range(G):
            for l in range(LT):
                mx_pass("a", 0, l, g)
        done = set(used)

        queues = [
            (engine, [(w[:-2], int(w[-2]), int(w[-1])) for w in order.split()])
            for engine, order in (("tensor", PE_ORDER), ("scalar", ACT_ORDER), ("vector", DVE_ORDER), ("sync", SP_ORDER))
        ]
        while any(queue for engine, queue in queues):
            moved = False
            for engine, queue in queues:
                while queue:
                    kind, n, l = queue[0]
                    wanted = needs(kind, n, l)
                    if engine == "tensor" and len(used) >= BANKS:
                        old = used[len(used) - BANKS]
                        wanted = wanted + [(empties[old[0]], old[1], old[2])]
                    if not all(w in done for w in wanted):
                        break
                    if engine == "tensor":
                        held[kind, n, l] = banks[len(used) % BANKS]
                        used.append((kind, n, l))
                    emit(engine, kind, n, l)
                    done.add(("cast" if kind == "mulb" else kind, n, l))
                    queue.pop(0)
                    moved = True
            assert moved
